import numpy as np
import ml_dtypes


def mxq(x, axis, fmt="e4m3"):
    dtype, down = {"e4m3": (ml_dtypes.float8_e4m3fn, 7), "e5m2": (ml_dtypes.float8_e5m2, 14)}[fmt]
    v = np.moveaxis(np.asarray(x, np.float32).astype(ml_dtypes.bfloat16).astype(np.float64), axis, -1)
    blocks = v.reshape(v.shape[:-1] + (-1, 32))
    amax = np.abs(blocks).max(-1, keepdims=True)
    byte = np.maximum(np.where(amax > 0, np.frexp(amax)[1] - 1 + 127, 0) - down, 1)
    scale = np.exp2(byte - 127.0)
    codes = (blocks / scale).astype(np.float32).astype(dtype).astype(np.float64)
    return np.moveaxis((codes * scale).reshape(v.shape), -1, axis)


WIDE = False


def mx_kscale(k):
    if not WIDE:
        return np.ones(k)
    levels = np.array([10, -10, 5, -5, 0])
    if k % 512:
        return np.exp2(np.random.permutation(np.resize(levels, k // 32))).repeat(32)
    a = np.empty((k // 512, 16))
    for p in range(k // 512):
        a[p, :8] = np.random.permutation(np.resize(levels, 8))
        for g in range(8):
            far = levels[np.abs(levels - a[p, g]) >= 10]
            a[p, g + 8] = far[np.random.randint(len(far))]
    return np.exp2(a.ravel()).repeat(32)


def f64(x):
    return np.asarray(x).astype(np.float64)


def striped(idx):
    return np.tile(np.asarray(idx).reshape(-1, 16).T, (8, 1)).astype(np.uint16)


def unstriped(offs):
    return offs[:16].T.reshape(-1).astype(np.int64)


E2M1 = np.array([0.0, 0.5, 1.0, 1.5, 2.0, 3.0, 4.0, 6.0, -0.0, -0.5, -1.0, -1.5, -2.0, -3.0, -4.0, -6.0])


def pack_weight(w, fmt):
    k, n = w.shape
    w = f64(np.asarray(w, np.float32).astype(ml_dtypes.bfloat16)).reshape(k // 32, 32, n)
    amax = np.abs(w).max(1)
    if fmt == "e4m3":
        byte = np.frexp(amax)[1] - 1 + 127 - 7
    else:
        mant, ex = np.frexp(amax / 6.0)
        byte = np.where(mant > 0.5, ex, ex - 1) + 127
    byte = np.clip(np.where(amax > 0, byte, 1), 1, 254)
    scaled = (w * np.exp2(127.0 - byte)[:, None, :]).reshape(k, n).astype(np.float32)
    by_word = np.ascontiguousarray(scaled.reshape(k // 512, 128, 4, n).transpose(0, 1, 3, 2))
    if fmt == "e4m3":
        words = by_word.astype(ml_dtypes.float8_e4m3fn).view(np.uint8)
    else:
        c = by_word.astype(ml_dtypes.float4_e2m1fn).view(np.uint8) & 0xF
        words = (c[..., 0::2] | (c[..., 1::2] << 4)).reshape(k // 512, 128, 2 * n)
    return np.ascontiguousarray(words), np.ascontiguousarray(byte.astype(np.uint8).reshape(k // 512, 16, n))


def unpack_weight(words, scales, fmt):
    g, _, n = scales.shape
    words = np.ascontiguousarray(words).reshape(g, 128, n, -1)
    if fmt == "e4m3":
        vals = words.view(ml_dtypes.float8_e4m3fn).astype(np.float64)
    else:
        nib = np.empty((g, 128, n, 4), np.uint8)
        nib[..., 0::2] = words & 0xF
        nib[..., 1::2] = words >> 4
        vals = E2M1[nib]
    vals = vals * np.repeat(np.exp2(scales.astype(np.float64) - 127.0), 8, axis=1)[..., None]
    return vals.transpose(0, 1, 3, 2).reshape(g * 512, n)


def sigmoid(v):
    return 1.0 / (1.0 + np.exp(-v))


D, E, T, I, Q = 512, 512, 2048, 512, 128


def setup_inputs():
    n = np.random.standard_normal
    idx = np.random.permutation(T)[:I]
    fd = mx_kscale(D)
    fe = mx_kscale(E)
    keysp = pack_weight(n((D, T)) / fd[:, None], "e2m1")
    valsp = pack_weight(n((E, T)) / fe[:, None], "e2m1")
    return {
        "query": (n((D, Q)) * 0.8 / np.sqrt(D) * fd[:, None]).astype(np.float32),
        "keys_words": keysp[0],
        "keys_scales": keysp[1],
        "th": (np.random.uniform(0.4, 1.0, (Q, 1))).astype(np.float32),
        "gout": (n((E, Q)) * 1 / np.sqrt(E) * fe[:, None]).astype(np.float32),
        "vals_words": valsp[0],
        "vals_scales": valsp[1],
        "base": (0.5 * n((Q, I))).astype(np.float32),
        "offs": striped(idx),
    }


def reference(query, keys_words, keys_scales, th, gout, vals_words, vals_scales, base, offs):
    idx = unstriped(offs)
    keysu = unpack_weight(keys_words, keys_scales, "e2m1")
    valsu = unpack_weight(vals_words, vals_scales, "e2m1")
    queryq = mxq(f64(query), 0, "e4m3")
    keysidxg = keysu[:, idx]
    a = queryq.T @ keysidxg
    e1s = sigmoid((f64(th) - np.mean(np.square(a), axis=1, keepdims=True)) * 4.0)
    p = np.exp(a - np.max(a, axis=1, keepdims=True))
    z = np.sum(p, axis=1, keepdims=True)
    goutq = mxq(f64(gout), 0, "e4m3")
    valsidxg = valsu[:, idx]
    c0 = goutq.T @ valsidxg
    dz = np.sum(c0 * (1.0 - e1s) * p / np.square(z) * (-1.0), axis=1, keepdims=True)
    dp = c0 * (1.0 - e1s) / z + dz
    de1s = np.sum(c0, axis=1, keepdims=True) / 512.0 - np.sum(c0 * p / z, axis=1, keepdims=True)
    da = dp * p + de1s * e1s * (1.0 - e1s) * 4.0 * (-1.0) / 512.0 * a * 2.0
    hda = da * 512.0 * 2.0 * 512.0
    hde1s = np.sum(hda * 2.0 * a, axis=1, keepdims=True) / 512.0 * (-1.0) * 4.0 * (1.0 - e1s) * e1s
    hdp = hda * p
    hdz = np.sum(hdp, axis=1, keepdims=True)
    hz = np.sum(hde1s * (-1.0) * c0 * p / np.square(z) * (-1.0), axis=1, keepdims=True) + np.sum(hdp * c0 * (1.0 - e1s) / np.square(z) * (-1.0), axis=1, keepdims=True) + np.sum(hdz * (-1.0) * c0 * (1.0 - e1s) * p / np.square(np.square(z)) * (-1.0), axis=1, keepdims=True) * z * 2.0
    hp = hda * dp + hde1s * (-1.0) * c0 / z + hdz * (-1.0) / np.square(z) * c0 * (1.0 - e1s) + hz
    he1s = np.sum(hda * 2.0 * a, axis=1, keepdims=True) / 512.0 * (-1.0) * 4.0 * (1.0 - e1s) * de1s - np.sum(hda * 2.0 * a, axis=1, keepdims=True) / 512.0 * (-1.0) * 4.0 * de1s * e1s - np.sum(hdp / z * c0, axis=1, keepdims=True) - np.sum(hdz * (-1.0) / np.square(z) * p * c0, axis=1, keepdims=True)
    ha = hda * 2.0 * de1s * e1s * (1.0 - e1s) * 4.0 * (-1.0) / 512.0 + hp * p + he1s * e1s * (1.0 - e1s) * 4.0 * (-1.0) / 512.0 * a * 2.0
    y = ha + f64(base)
    return y

@@ -1,0 +1,166 @@
+import math
+from contextlib import ExitStack
+
+import concourse.mybir as mybir
+
+D, E, T, I, Q = 512, 512, 2048, 512, 128
+FLOPS = 2 * Q * I * (D + E)
+
+F32 = mybir.dt.float32
+BF16 = mybir.dt.bfloat16
+I32 = mybir.dt.int32
+U32 = mybir.dt.uint32
+U16 = mybir.dt.uint16
+U8 = mybir.dt.uint8
+FP8X4 = mybir.dt.float8_e4m3fn_x4
+FP4X4 = mybir.dt.float4_e2m1fn_x4
+ALU = mybir.AluOpType
+ACT = mybir.ActivationFunctionType
+AX = mybir.AxisListType
+
+P = 128
+ROOT_H = math.sqrt(2.0 * 512 * 512)
+HALVES = (slice(0, I // 2), slice(I // 2, I))
+
+
+def tile_attend_gpevenbyspread_kernel(tc, query, keys_words, keys_scales, th, gout, vals_words, vals_scales, base, offs, out):
+    nc = tc.nc
+    with ExitStack() as ctx:
+        sb = ctx.enter_context(tc.tile_pool(name="sb", bufs=1))
+        ps = ctx.enter_context(tc.psum_pool(name="ps", bufs=1))
+
+        def wide(name, dtype=F32, cols=I):
+            return sb.tile([P, cols], dtype, name=name, align_bytes=64)
+
+        def col(name, cols=1):
+            return sb.tile([P, cols], F32, name=name)
+
+        def load_scales(plane, scales):
+            for quad in range(4):
+                nc.sync.dma_start(plane[32 * quad : 32 * quad + 4, :].bitcast(I32), scales[0, 4 * quad : 4 * quad + 4, :].bitcast(I32))
+
+        offsets = sb.tile([P, I // 16], U16, name="offsets")
+        k_pool = sb.tile([P, T], U16, name="k_pool", tag="k_pool", align_bytes=64)
+        ks_pool, vs_pool = sb.tile([P, T], U8, name="ks_pool", tag="ks_pool", align_bytes=64), sb.tile([P, T], U8, name="vs_pool", tag="vs_pool", align_bytes=64)
+        q_raw = sb.tile([P, 4, Q], F32, name="q_raw", tag="q_raw")
+
+        warm_in = sb.tile([P, 1], F32, name="warm_in", tag="v_pool", align_bytes=64)
+        warm_out = sb.tile([P, 1], F32, name="warm_out", tag="g_raw")
+        nc.vector.memset(ks_pool[:].bitcast(I32), 0)
+        nc.gpsimd.memset(warm_in[:], 0.0)
+        nc.vector.memset(vs_pool[:].bitcast(I32), 0)
+
+        nc.sync.dma_start(offsets[:], offs)
+        nc.scalar.dma_start(k_pool[:].bitcast(I32), keys_words[0].bitcast(I32))
+        nc.scalar.dma_start(q_raw[:], query.rearrange("(p j) q -> p j q", j=4))
+        load_scales(ks_pool, keys_scales)
+        nc.scalar.activation(warm_out[:], warm_in[:], ACT.Exp)
+        load_scales(vs_pool, vals_scales)
+        v_pool = sb.tile([P, T], U16, name="v_pool", tag="v_pool", align_bytes=64)
+        g_raw = sb.tile([P, 4, Q], F32, name="g_raw", tag="g_raw")
+        nc.sync.dma_start(v_pool[:].bitcast(I32), vals_words[0].bitcast(I32))
+        nc.sync.dma_start(g_raw[:], gout.rearrange("(p j) q -> p j q", j=4))
+
+        def interleave(raw, name):
+            grouped = sb.tile([P, Q, 4], BF16, name=name, tag=name, align_bytes=64)
+            nc.scalar.copy(grouped[:], raw[:].rearrange("p j q -> p q j"))
+            return grouped
+
+        def quantize(grouped, name):
+            codes, scales = wide(name + "_codes", U32, Q), wide(name + "_scales", U8, Q)
+            nc.vector.quantize_mx(codes[:].bitcast(FP8X4), scales[:], grouped[:].rearrange("p q j -> p (q j)"))
+            return codes, scales
+
+        def gather(pool_tile, dtype, name, tag=None):
+            picked = sb.tile([P, I], dtype, name=name, tag=tag or name, align_bytes=64)
+            nc.vector.tensor_copy(picked[:], pool_tile[:].indirect(offsets[:]))
+            return picked
+
+        def product(name, lhs, words, scales):
+            bank = ps.tile([P, I], F32, name=name)
+            nc.tensor.matmul_mx(bank[:], lhsT=lhs[0][:].bitcast(FP8X4), lhsT_scale=lhs[1][:], rhs=words[:].bitcast(FP4X4), rhs_scale=scales[:], start=True, stop=True)
+            return bank
+
+        q_grouped = interleave(q_raw, "q_grouped")
+        k_words = gather(k_pool, U16, "k_words")
+        k_scales = gather(ks_pool, U8, "k_scales")
+        a = product("a", quantize(q_grouped, "q"), k_words, k_scales)
+
+        base_sb = sb.tile([P, I], F32, name="base_sb", tag="k_pool", align_bytes=64)
+        th_sb = sb.tile([P, 1], F32, name="th_sb", tag="q_raw")
+        nc.sync.dma_start(th_sb[:], th)
+        nc.sync.dma_start(base_sb[:], base)
+        g_grouped = interleave(g_raw, "g_grouped")
+        th2n = col("th2n")
+        nc.scalar.activation(th2n[:], th_sb[:], ACT.Copy, scale=-2.0)
+        v_scales = gather(vs_pool, U8, "v_scales", "q_grouped")
+
+        saa, tn, neg_max, z, sar = col("saa"), col("tn"), col("neg_max"), col("z"), col("sar")
+        junk0, p, r = wide("junk0"), wide("p"), wide("r")
+        neg_a = sb.tile([P, I], F32, name="neg_a", tag="vs_pool", align_bytes=64)
+        nc.vector.tensor_scalar(neg_a[:], a[:], -1.0, None, ALU.mult, ALU.min, accum_out=neg_max[:])
+        nc.scalar.activation(p[:], neg_a[:], ACT.Exp, scale=-1.0, bias=neg_max[:], accum_out=z[:])
+        nc.scalar.activation(junk0[:], neg_a[:], ACT.Square, accum_out=saa[:])
+        nc.scalar.activation(tn[:], saa[:], ACT.Tanh, scale=1.0 / 256, bias=th2n[:])
+
+        v_words = gather(v_pool, U16, "v_words")
+        c = product("c", quantize(g_grouped, "g"), v_words, v_scales)
+
+        reuse = sb.tile([P, I + 8], F32, name="reuse", tag="v_pool", align_bytes=64)
+        junk1, rz = reuse[:, :I], reuse[:, I : I + 1]
+        nc.vector.reciprocal(rz, z[:])
+        nc.scalar.activation(r[:], p[:], ACT.Copy, scale=rz)
+        nc.vector.scalar_tensor_tensor(junk1, a[:], rz, p[:], ALU.mult, ALU.mult, accum_out=sar[:])
+
+        def affine(dst, x, m, b):
+            nc.scalar.activation(dst, x, ACT.Copy if isinstance(b, float) else ACT.Identity, scale=m, bias=b)
+
+        scu, s64, s128, tt, g1 = (col(n) for n in ("scu", "s64", "s128", "tt", "g1"))
+        ell = col("ell", 2)
+        affine(tt[:], tn[:], tn[:], -1.0)
+        affine(scu[:], tn[:], ROOT_H / 2, ROOT_H / 2)
+        affine(s64[:], tn[:], -1.0 / 128, 1.0 / 128)
+        affine(s128[:], tn[:], -1.0 / 256, 1.0 / 256)
+        affine(ell[:, 1:2], tn[:], -1.0 / 64, 0.0)
+        affine(g1[:], tt[:], ROOT_H / 131072, 0.0)
+        affine(ell[:, 0:1], sar[:], -0.5, 0.5)
+
+        y, nw, wa, junk2, junk3, junk4 = (wide(n) for n in ("y", "nw", "wa", "junk2", "junk3", "junk4"))
+        cbar, nd, sq, rr = col("cbar"), col("nd"), col("sq"), col("rr")
+        ra_part = [col("ra0"), col("ra1")]
+        nc.vector.scalar_tensor_tensor(y[:], c[:], rz, p[:], ALU.mult, ALU.mult, accum_out=cbar[:])
+        nc.scalar.activation(junk2[:], c[:], ACT.Identity, scale=-1.0, bias=cbar[:], accum_out=nd[:])
+        for h in HALVES:
+            nc.vector.scalar_tensor_tensor(nw[:, h], r[:, h], cbar[:], y[:, h], ALU.mult, ALU.subtract)
+        gp, gl = col("gp"), col("gl", 2)
+        nc.scalar.activation(gp[:], nd[:], ACT.Copy, scale=g1[:])
+        nc.scalar.activation(junk3[:], nw[:], ACT.Square, scale=scu[:], accum_out=sq[:])
+        for h, part in zip(HALVES, ra_part):
+            nc.vector.scalar_tensor_tensor(wa[:, h], nw[:, h], scu[:], a[:, h], ALU.mult, ALU.mult, accum_out=part[:])
+        nc.vector.scalar_tensor_tensor(junk4[:], nw[:], scu[:], r[:], ALU.mult, ALU.mult, accum_out=rr[:])
+
+        g2, a0, u0, aa, ue, n1, t2, theta, nmu, mu2 = (col(n) for n in ("g2", "a0", "u0", "aa", "ue", "n1", "t2", "theta", "nmu", "mu2"))
+        affine(a0[:], gp[:], saa[:], ra_part[0][:])
+        affine(u0[:], ra_part[0][:], gp[:], sq[:])
+        affine(gl[:], ell[:], gp[:], 0.0)
+        nc.scalar.activation(g2[:], gp[:], ACT.Square)
+        affine(aa[:], ra_part[1][:], 1.0, a0[:])
+        affine(ue[:], ra_part[1][:], gp[:], u0[:])
+        affine(n1[:], aa[:], s128[:], gl[:, 0:1])
+        affine(t2[:], aa[:], gl[:, 1:2], g2[:])
+        affine(nmu[:], rr[:], -0.5, n1[:])
+        affine(theta[:], ue[:], s64[:], t2[:])
+
+        x1, x2, x3, sqr, res = (wide(n) for n in ("x1", "x2", "x3", "sqr", "res"))
+        for h in HALVES:
+            nc.scalar.activation(sqr[:, h], nw[:, h], ACT.Square, scale=scu[:], bias=nmu[:])
+        nc.scalar.activation(mu2[:], nmu[:], ACT.Square)
+        for h in HALVES:
+            nc.vector.scalar_tensor_tensor(x1[:, h], wa[:, h], gp[:], base_sb[:, h], ALU.mult, ALU.add)
+        for h in HALVES:
+            nc.vector.scalar_tensor_tensor(x2[:, h], r[:, h], ue[:], x1[:, h], ALU.mult, ALU.subtract)
+        for h in HALVES:
+            nc.vector.scalar_tensor_tensor(x3[:, h], a[:, h], theta[:], x2[:, h], ALU.mult, ALU.subtract)
+        for h in HALVES:
+            nc.vector.scalar_tensor_tensor(res[:, h], sqr[:, h], mu2[:], x3[:, h], ALU.subtract, ALU.add)
+            nc.sync.dma_start(out[:, h], res[:, h])

@@ -41,33 +41,38 @@ def tile_attend_gpevenbyspread_kernel(tc, query, keys_words, keys_scales, th, go
 
         offsets = sb.tile([P, I // 16], U16, name="offsets")
         k_pool = sb.tile([P, T], U16, name="k_pool", tag="k_pool", align_bytes=64)
-        ks_pool, vs_pool = sb.tile([P, T], U8, name="ks_pool", tag="ks_pool", align_bytes=64), sb.tile([P, T], U8, name="vs_pool", tag="vs_pool", align_bytes=64)
+        ks_pool = sb.tile([P, T], U8, name="ks_pool", tag="ks_pool", align_bytes=64)
+        warm_sum = sb.tile([P, 1], F32, name="warm_sum", tag="vs_pool", align_bytes=64)
         q_raw = sb.tile([P, 4, Q], F32, name="q_raw", tag="q_raw")
 
         warm_in = sb.tile([P, 1], F32, name="warm_in", tag="v_pool", align_bytes=64)
         warm_out = sb.tile([P, 1], F32, name="warm_out", tag="g_raw")
         nc.vector.memset(ks_pool[:].bitcast(I32), 0)
-        nc.gpsimd.memset(warm_in[:], 0.0)
-        nc.vector.memset(vs_pool[:].bitcast(I32), 0)
+        nc.vector.memset(warm_in[:], 0.0)
 
         nc.sync.dma_start(offsets[:], offs)
+        th_sb = col("th_sb")
+        nc.sync.dma_start(th_sb[:], th)
         nc.scalar.dma_start(k_pool[:].bitcast(I32), keys_words[0].bitcast(I32))
         nc.scalar.dma_start(q_raw[:], query.rearrange("(p j) q -> p j q", j=4))
         load_scales(ks_pool, keys_scales)
-        nc.scalar.activation(warm_out[:], warm_in[:], ACT.Exp)
-        load_scales(vs_pool, vals_scales)
+        nc.scalar.activation(warm_out[:], warm_in[:], ACT.Exp, accum_out=warm_sum[:])
         v_pool = sb.tile([P, T], U16, name="v_pool", tag="v_pool", align_bytes=64)
         g_raw = sb.tile([P, 4, Q], F32, name="g_raw", tag="g_raw")
         nc.sync.dma_start(v_pool[:].bitcast(I32), vals_words[0].bitcast(I32))
         nc.sync.dma_start(g_raw[:], gout.rearrange("(p j) q -> p j q", j=4))
+        vs_pool = sb.tile([P, T], U8, name="vs_pool", tag="vs_pool", align_bytes=64)
+        nc.gpsimd.memset(vs_pool[:].bitcast(I32), 0)
+        load_scales(vs_pool, vals_scales)
 
         def interleave(raw, name):
             grouped = sb.tile([P, Q, 4], BF16, name=name, tag=name, align_bytes=64)
             nc.scalar.copy(grouped[:], raw[:].rearrange("p j q -> p q j"))
             return grouped
 
-        def quantize(grouped, name):
-            codes, scales = wide(name + "_codes", U32, Q), wide(name + "_scales", U8, Q)
+        def quantize(grouped, name, tag=None):
+            codes = wide(name + "_codes", U32, Q)
+            scales = sb.tile([P, Q], U8, name=name + "_scales", tag=tag or name + "_scales", align_bytes=64)
             nc.vector.quantize_mx(codes[:].bitcast(FP8X4), scales[:], grouped[:].rearrange("p q j -> p (q j)"))
             return codes, scales
 
@@ -84,30 +89,30 @@ def tile_attend_gpevenbyspread_kernel(tc, query, keys_words, keys_scales, th, go
         q_grouped = interleave(q_raw, "q_grouped")
         k_words = gather(k_pool, U16, "k_words")
         k_scales = gather(ks_pool, U8, "k_scales")
-        a = product("a", quantize(q_grouped, "q"), k_words, k_scales)
+        a = product("a", quantize(q_grouped, "q", "ks_pool"), k_words, k_scales)
 
-        base_sb = sb.tile([P, I], F32, name="base_sb", tag="k_pool", align_bytes=64)
-        th_sb = sb.tile([P, 1], F32, name="th_sb", tag="q_raw")
-        nc.sync.dma_start(th_sb[:], th)
+        base_sb = sb.tile([P, I], F32, name="base_sb", tag="k_words", align_bytes=64)
         nc.sync.dma_start(base_sb[:], base)
         g_grouped = interleave(g_raw, "g_grouped")
         th2n = col("th2n")
         nc.scalar.activation(th2n[:], th_sb[:], ACT.Copy, scale=-2.0)
-        v_scales = gather(vs_pool, U8, "v_scales", "q_grouped")
+        v_words = gather(v_pool, U16, "v_words")
 
         saa, tn, neg_max, z, sar = col("saa"), col("tn"), col("neg_max"), col("z"), col("sar")
-        junk0, p, r = wide("junk0"), wide("p"), wide("r")
-        neg_a = sb.tile([P, I], F32, name="neg_a", tag="vs_pool", align_bytes=64)
+        junk0, r = wide("junk0"), wide("r")
+        p = sb.tile([P, I], F32, name="p", tag="g_raw")
+        neg_a = sb.tile([P, I], F32, name="neg_a", tag="v_pool", align_bytes=64)
         nc.vector.tensor_scalar(neg_a[:], a[:], -1.0, None, ALU.mult, ALU.min, accum_out=neg_max[:])
         nc.scalar.activation(p[:], neg_a[:], ACT.Exp, scale=-1.0, bias=neg_max[:], accum_out=z[:])
         nc.scalar.activation(junk0[:], neg_a[:], ACT.Square, accum_out=saa[:])
         nc.scalar.activation(tn[:], saa[:], ACT.Tanh, scale=1.0 / 256, bias=th2n[:])
 
-        v_words = gather(v_pool, U16, "v_words")
-        c = product("c", quantize(g_grouped, "g"), v_words, v_scales)
+        g_q = quantize(g_grouped, "g")
+        v_scales = gather(vs_pool, U8, "v_scales")
+        c = product("c", g_q, v_words, v_scales)
 
-        reuse = sb.tile([P, I + 8], F32, name="reuse", tag="v_pool", align_bytes=64)
-        junk1, rz = reuse[:, :I], reuse[:, I : I + 1]
+        rz = sb.tile([P, 1], F32, name="rz", tag="vs_pool", align_bytes=64)[:]
+        junk1 = sb.tile([P, I], F32, name="junk1", tag="g_grouped", align_bytes=64)[:]
         nc.vector.reciprocal(rz, z[:])
         nc.scalar.activation(r[:], p[:], ACT.Copy, scale=rz)
         nc.vector.scalar_tensor_tensor(junk1, a[:], rz, p[:], ALU.mult, ALU.mult, accum_out=sar[:])

@@ -47,15 +47,15 @@ def tile_attend_gpevenbyspread_kernel(tc, query, keys_words, keys_scales, th, go
 
         warm_in = sb.tile([P, 1], F32, name="warm_in", tag="v_pool", align_bytes=64)
         warm_out = sb.tile([P, 1], F32, name="warm_out", tag="g_raw")
-        nc.vector.memset(ks_pool[:].bitcast(I32), 0)
         nc.vector.memset(warm_in[:], 0.0)
 
         nc.sync.dma_start(offsets[:], offs)
-        th_sb = col("th_sb")
-        nc.sync.dma_start(th_sb[:], th)
-        nc.scalar.dma_start(k_pool[:].bitcast(I32), keys_words[0].bitcast(I32))
-        nc.scalar.dma_start(q_raw[:], query.rearrange("(p j) q -> p j q", j=4))
-        load_scales(ks_pool, keys_scales)
+        for quad in range(4):
+            rows = keys_scales[0, 4 * quad : 4 * quad + 4, :].bitcast(I32)
+            queue = nc.scalar if quad < 2 else nc.sync
+            queue.dma_start(ks_pool[32 * quad : 32 * quad + 32, :].bitcast(I32), rows.unsqueeze(0).to_broadcast([8, 4, T // 4]))
+        nc.sync.dma_start(k_pool[:].bitcast(I32), keys_words[0].bitcast(I32))
+        nc.sync.dma_start(q_raw[:], query.rearrange("(p j) q -> p j q", j=4))
         nc.scalar.activation(warm_out[:], warm_in[:], ACT.Exp, accum_out=warm_sum[:])
         v_pool = sb.tile([P, T], U16, name="v_pool", tag="v_pool", align_bytes=64)
         g_raw = sb.tile([P, 4, Q], F32, name="g_raw", tag="g_raw")
@@ -87,11 +87,13 @@ def tile_attend_gpevenbyspread_kernel(tc, query, keys_words, keys_scales, th, go
             return bank
 
         q_grouped = interleave(q_raw, "q_grouped")
-        k_words = gather(k_pool, U16, "k_words")
         k_scales = gather(ks_pool, U8, "k_scales")
-        a = product("a", quantize(q_grouped, "q", "ks_pool"), k_words, k_scales)
+        k_words = gather(k_pool, U16, "k_words")
+        a = product("a", quantize(q_grouped, "q", "k_pool"), k_words, k_scales)
 
         base_sb = sb.tile([P, I], F32, name="base_sb", tag="k_words", align_bytes=64)
+        th_sb = sb.tile([P, 1], F32, name="th_sb", tag="q_raw")
+        nc.sync.dma_start(th_sb[:], th)
         nc.sync.dma_start(base_sb[:], base)
         g_grouped = interleave(g_raw, "g_grouped")
         th2n = col("th2n")
@@ -107,15 +109,18 @@ def tile_attend_gpevenbyspread_kernel(tc, query, keys_words, keys_scales, th, go
         nc.scalar.activation(junk0[:], neg_a[:], ACT.Square, accum_out=saa[:])
         nc.scalar.activation(tn[:], saa[:], ACT.Tanh, scale=1.0 / 256, bias=th2n[:])
 
-        g_q = quantize(g_grouped, "g")
-        v_scales = gather(vs_pool, U8, "v_scales")
-        c = product("c", g_q, v_words, v_scales)
+        g_codes, g_scales = quantize(g_grouped, "g")
+        c = ps.tile([P, I], F32, name="c")
+        for h, tag in zip(HALVES, ("v_scales", "g_grouped")):
+            v_scales = sb.tile([P, I // 2], U8, name="v_scales", tag=tag, align_bytes=64)
+            nc.vector.tensor_copy(v_scales[:], vs_pool[:].indirect(offsets[:, h.start // 16 : h.stop // 16]))
+            nc.tensor.matmul_mx(c[:, h], lhsT=g_codes[:].bitcast(FP8X4), lhsT_scale=g_scales[:], rhs=v_words[:, h].bitcast(FP4X4), rhs_scale=v_scales[:], start=True, stop=True)
 
-        rz = sb.tile([P, 1], F32, name="rz", tag="vs_pool", align_bytes=64)[:]
-        junk1 = sb.tile([P, I], F32, name="junk1", tag="g_grouped", align_bytes=64)[:]
+        reuse = sb.tile([P, I + 8], F32, name="reuse", tag="vs_pool", align_bytes=64)
+        junk1, rz = reuse[:, :I], reuse[:, I : I + 1]
         nc.vector.reciprocal(rz, z[:])
         nc.scalar.activation(r[:], p[:], ACT.Copy, scale=rz)
-        nc.vector.scalar_tensor_tensor(junk1, a[:], rz, p[:], ALU.mult, ALU.mult, accum_out=sar[:])
+        nc.vector.scalar_tensor_tensor(junk1, a[:], -0.5, p[:], ALU.mult, ALU.mult, accum_out=sar[:])
 
         def affine(dst, x, m, b):
             nc.scalar.activation(dst, x, ACT.Copy if isinstance(b, float) else ACT.Identity, scale=m, bias=b)
@@ -128,7 +133,7 @@ def tile_attend_gpevenbyspread_kernel(tc, query, keys_words, keys_scales, th, go
         affine(s128[:], tn[:], -1.0 / 256, 1.0 / 256)
         affine(ell[:, 1:2], tn[:], -1.0 / 64, 0.0)
         affine(g1[:], tt[:], ROOT_H / 131072, 0.0)
-        affine(ell[:, 0:1], sar[:], -0.5, 0.5)
+        affine(ell[:, 0:1], sar[:], rz, 0.5)
 
         y, nw, wa, junk2, junk3, junk4 = (wide(n) for n in ("y", "nw", "wa", "junk2", "junk3", "junk4"))
         cbar, nd, sq, rr = col("cbar"), col("nd"), col("sq"), col("rr")

import math
from contextlib import ExitStack

import concourse.mybir as mybir

D, E, T, I, Q = 512, 512, 2048, 512, 128
FLOPS = 2 * Q * I * (D + E)

F32 = mybir.dt.float32
BF16 = mybir.dt.bfloat16
I32 = mybir.dt.int32
U32 = mybir.dt.uint32
U16 = mybir.dt.uint16
U8 = mybir.dt.uint8
FP8X4 = mybir.dt.float8_e4m3fn_x4
FP4X4 = mybir.dt.float4_e2m1fn_x4
ALU = mybir.AluOpType
ACT = mybir.ActivationFunctionType
AX = mybir.AxisListType

P = 128
ROOT_H = math.sqrt(2.0 * 512 * 512)
HALVES = (slice(0, I // 2), slice(I // 2, I))


def tile_attend_gpevenbyspread_kernel(tc, query, keys_words, keys_scales, th, gout, vals_words, vals_scales, base, offs, out):
    nc = tc.nc
    with ExitStack() as ctx:
        sb = ctx.enter_context(tc.tile_pool(name="sb", bufs=1))
        ps = ctx.enter_context(tc.psum_pool(name="ps", bufs=1))

        def wide(name, dtype=F32, cols=I):
            return sb.tile([P, cols], dtype, name=name, align_bytes=64)

        def col(name, cols=1):
            return sb.tile([P, cols], F32, name=name)

        def load_scales(plane, scales):
            for quad in range(4):
                nc.sync.dma_start(plane[32 * quad : 32 * quad + 4, :].bitcast(I32), scales[0, 4 * quad : 4 * quad + 4, :].bitcast(I32))

        offsets = sb.tile([P, I // 16], U16, name="offsets")
        k_pool = sb.tile([P, T], U16, name="k_pool", tag="k_pool", align_bytes=64)
        ks_pool = sb.tile([P, T], U8, name="ks_pool", tag="ks_pool", align_bytes=64)
        warm_sum = sb.tile([P, 1], F32, name="warm_sum", tag="vs_pool", align_bytes=64)
        q_raw = sb.tile([P, 4, Q], F32, name="q_raw", tag="q_raw")

        warm_in = sb.tile([P, 1], F32, name="warm_in", tag="v_pool", align_bytes=64)
        warm_out = sb.tile([P, 1], F32, name="warm_out", tag="g_raw")
        nc.vector.memset(warm_in[:], 0.0)

        nc.sync.dma_start(offsets[:], offs)
        for quad in range(4):
            rows = keys_scales[0, 4 * quad : 4 * quad + 4, :].bitcast(I32)
            queue = nc.scalar if quad < 2 else nc.sync
            queue.dma_start(ks_pool[32 * quad : 32 * quad + 32, :].bitcast(I32), rows.unsqueeze(0).to_broadcast([8, 4, T // 4]))
        nc.sync.dma_start(k_pool[:].bitcast(I32), keys_words[0].bitcast(I32))
        nc.sync.dma_start(q_raw[:], query.rearrange("(p j) q -> p j q", j=4))
        nc.scalar.activation(warm_out[:], warm_in[:], ACT.Exp, accum_out=warm_sum[:])
        v_pool = sb.tile([P, T], U16, name="v_pool", tag="v_pool", align_bytes=64)
        g_raw = sb.tile([P, 4, Q], F32, name="g_raw", tag="g_raw")
        nc.sync.dma_start(v_pool[:].bitcast(I32), vals_words[0].bitcast(I32))
        nc.sync.dma_start(g_raw[:], gout.rearrange("(p j) q -> p j q", j=4))
        vs_pool = sb.tile([P, T], U8, name="vs_pool", tag="vs_pool", align_bytes=64)
        nc.gpsimd.memset(vs_pool[:].bitcast(I32), 0)
        load_scales(vs_pool, vals_scales)

        def interleave(raw, name):
            grouped = sb.tile([P, Q, 4], BF16, name=name, tag=name, align_bytes=64)
            nc.scalar.copy(grouped[:], raw[:].rearrange("p j q -> p q j"))
            return grouped

        def quantize(grouped, name, tag=None):
            codes = wide(name + "_codes", U32, Q)
            scales = sb.tile([P, Q], U8, name=name + "_scales", tag=tag or name + "_scales", align_bytes=64)
            nc.vector.quantize_mx(codes[:].bitcast(FP8X4), scales[:], grouped[:].rearrange("p q j -> p (q j)"))
            return codes, scales

        def gather(pool_tile, dtype, name, tag=None):
            picked = sb.tile([P, I], dtype, name=name, tag=tag or name, align_bytes=64)
            nc.vector.tensor_copy(picked[:], pool_tile[:].indirect(offsets[:]))
            return picked

        def product(name, lhs, words, scales):
            bank = ps.tile([P, I], F32, name=name)
            nc.tensor.matmul_mx(bank[:], lhsT=lhs[0][:].bitcast(FP8X4), lhsT_scale=lhs[1][:], rhs=words[:].bitcast(FP4X4), rhs_scale=scales[:], start=True, stop=True)
            return bank

        q_grouped = interleave(q_raw, "q_grouped")
        k_scales = gather(ks_pool, U8, "k_scales")
        k_words = gather(k_pool, U16, "k_words")
        a = product("a", quantize(q_grouped, "q", "k_pool"), k_words, k_scales)

        base_sb = sb.tile([P, I], F32, name="base_sb", tag="k_words", align_bytes=64)
        th_sb = sb.tile([P, 1], F32, name="th_sb", tag="q_raw")
        nc.sync.dma_start(th_sb[:], th)
        nc.sync.dma_start(base_sb[:], base)
        g_grouped = interleave(g_raw, "g_grouped")
        th2n = col("th2n")
        nc.scalar.activation(th2n[:], th_sb[:], ACT.Copy, scale=-2.0)
        v_words = gather(v_pool, U16, "v_words")

        saa, tn, neg_max, z, sar = col("saa"), col("tn"), col("neg_max"), col("z"), col("sar")
        junk0, r = wide("junk0"), wide("r")
        p = sb.tile([P, I], F32, name="p", tag="g_raw")
        neg_a = sb.tile([P, I], F32, name="neg_a", tag="v_pool", align_bytes=64)
        nc.vector.tensor_scalar(neg_a[:], a[:], -1.0, None, ALU.mult, ALU.min, accum_out=neg_max[:])
        nc.scalar.activation(p[:], neg_a[:], ACT.Exp, scale=-1.0, bias=neg_max[:], accum_out=z[:])
        nc.scalar.activation(junk0[:], neg_a[:], ACT.Square, accum_out=saa[:])
        nc.scalar.activation(tn[:], saa[:], ACT.Tanh, scale=1.0 / 256, bias=th2n[:])

        g_codes, g_scales = quantize(g_grouped, "g")
        c = ps.tile([P, I], F32, name="c")
        for h, tag in zip(HALVES, ("v_scales", "g_grouped")):
            v_scales = sb.tile([P, I // 2], U8, name="v_scales", tag=tag, align_bytes=64)
            nc.vector.tensor_copy(v_scales[:], vs_pool[:].indirect(offsets[:, h.start // 16 : h.stop // 16]))
            nc.tensor.matmul_mx(c[:, h], lhsT=g_codes[:].bitcast(FP8X4), lhsT_scale=g_scales[:], rhs=v_words[:, h].bitcast(FP4X4), rhs_scale=v_scales[:], start=True, stop=True)

        reuse = sb.tile([P, I + 8], F32, name="reuse", tag="vs_pool", align_bytes=64)
        junk1, rz = reuse[:, :I], reuse[:, I : I + 1]
        nc.vector.reciprocal(rz, z[:])
        nc.scalar.activation(r[:], p[:], ACT.Copy, scale=rz)
        nc.vector.scalar_tensor_tensor(junk1, a[:], -0.5, p[:], ALU.mult, ALU.mult, accum_out=sar[:])

        def affine(dst, x, m, b):
            nc.scalar.activation(dst, x, ACT.Copy if isinstance(b, float) else ACT.Identity, scale=m, bias=b)

        scu, s64, s128, tt, g1 = (col(n) for n in ("scu", "s64", "s128", "tt", "g1"))
        ell = col("ell", 2)
        affine(tt[:], tn[:], tn[:], -1.0)
        affine(scu[:], tn[:], ROOT_H / 2, ROOT_H / 2)
        affine(s64[:], tn[:], -1.0 / 128, 1.0 / 128)
        affine(s128[:], tn[:], -1.0 / 256, 1.0 / 256)
        affine(ell[:, 1:2], tn[:], -1.0 / 64, 0.0)
        affine(g1[:], tt[:], ROOT_H / 131072, 0.0)
        affine(ell[:, 0:1], sar[:], rz, 0.5)

        y, nw, wa, junk2, junk3, junk4 = (wide(n) for n in ("y", "nw", "wa", "junk2", "junk3", "junk4"))
        cbar, nd, sq, rr = col("cbar"), col("nd"), col("sq"), col("rr")
        ra_part = [col("ra0"), col("ra1")]
        nc.vector.scalar_tensor_tensor(y[:], c[:], rz, p[:], ALU.mult, ALU.mult, accum_out=cbar[:])
        nc.scalar.activation(junk2[:], c[:], ACT.Identity, scale=-1.0, bias=cbar[:], accum_out=nd[:])
        for h in HALVES:
            nc.vector.scalar_tensor_tensor(nw[:, h], r[:, h], cbar[:], y[:, h], ALU.mult, ALU.subtract)
        gp, gl = col("gp"), col("gl", 2)
        nc.scalar.activation(gp[:], nd[:], ACT.Copy, scale=g1[:])
        nc.scalar.activation(junk3[:], nw[:], ACT.Square, scale=scu[:], accum_out=sq[:])
        for h, part in zip(HALVES, ra_part):
            nc.vector.scalar_tensor_tensor(wa[:, h], nw[:, h], scu[:], a[:, h], ALU.mult, ALU.mult, accum_out=part[:])
        nc.vector.scalar_tensor_tensor(junk4[:], nw[:], scu[:], r[:], ALU.mult, ALU.mult, accum_out=rr[:])

        g2, a0, u0, aa, ue, n1, t2, theta, nmu, mu2 = (col(n) for n in ("g2", "a0", "u0", "aa", "ue", "n1", "t2", "theta", "nmu", "mu2"))
        affine(a0[:], gp[:], saa[:], ra_part[0][:])
        affine(u0[:], ra_part[0][:], gp[:], sq[:])
        affine(gl[:], ell[:], gp[:], 0.0)
        nc.scalar.activation(g2[:], gp[:], ACT.Square)
        affine(aa[:], ra_part[1][:], 1.0, a0[:])
        affine(ue[:], ra_part[1][:], gp[:], u0[:])
        affine(n1[:], aa[:], s128[:], gl[:, 0:1])
        affine(t2[:], aa[:], gl[:, 1:2], g2[:])
        affine(nmu[:], rr[:], -0.5, n1[:])
        affine(theta[:], ue[:], s64[:], t2[:])

        x1, x2, x3, sqr, res = (wide(n) for n in ("x1", "x2", "x3", "sqr", "res"))
        for h in HALVES:
            nc.scalar.activation(sqr[:, h], nw[:, h], ACT.Square, scale=scu[:], bias=nmu[:])
        nc.scalar.activation(mu2[:], nmu[:], ACT.Square)
        for h in HALVES:
            nc.vector.scalar_tensor_tensor(x1[:, h], wa[:, h], gp[:], base_sb[:, h], ALU.mult, ALU.add)
        for h in HALVES:
            nc.vector.scalar_tensor_tensor(x2[:, h], r[:, h], ue[:], x1[:, h], ALU.mult, ALU.subtract)
        for h in HALVES:
            nc.vector.scalar_tensor_tensor(x3[:, h], a[:, h], theta[:], x2[:, h], ALU.mult, ALU.subtract)
        for h in HALVES:
            nc.vector.scalar_tensor_tensor(res[:, h], sqr[:, h], mu2[:], x3[:, h], ALU.subtract, ALU.add)
            nc.sync.dma_start(out[:, h], res[:, h])
